import numpy as np
import ml_dtypes


def mxq(x, axis, fmt="e4m3"):
    dtype, down = {"e4m3": (ml_dtypes.float8_e4m3fn, 7), "e5m2": (ml_dtypes.float8_e5m2, 14)}[fmt]
    v = np.moveaxis(np.asarray(x, np.float32).astype(ml_dtypes.bfloat16).astype(np.float64), axis, -1)
    blocks = v.reshape(v.shape[:-1] + (-1, 32))
    amax = np.abs(blocks).max(-1, keepdims=True)
    byte = np.maximum(np.where(amax > 0, np.frexp(amax)[1] - 1 + 127, 0) - down, 1)
    scale = np.exp2(byte - 127.0)
    codes = (blocks / scale).astype(np.float32).astype(dtype).astype(np.float64)
    return np.moveaxis((codes * scale).reshape(v.shape), -1, axis)


WIDE = False


def mx_kscale(k):
    if not WIDE:
        return np.ones(k)
    levels = np.array([10, -10, 5, -5, 0])
    if k % 512:
        return np.exp2(np.random.permutation(np.resize(levels, k // 32))).repeat(32)
    a = np.empty((k // 512, 16))
    for p in range(k // 512):
        a[p, :8] = np.random.permutation(np.resize(levels, 8))
        for g in range(8):
            far = levels[np.abs(levels - a[p, g]) >= 10]
            a[p, g + 8] = far[np.random.randint(len(far))]
    return np.exp2(a.ravel()).repeat(32)


def f64(x):
    return np.asarray(x).astype(np.float64)


def striped(idx):
    return np.tile(idx.reshape(-1, 16).T, (8, 1)).astype(np.uint16)


def unstriped(offs):
    return offs[:16].T.reshape(-1).astype(np.int64)


E2M1 = np.array([0.0, 0.5, 1.0, 1.5, 2.0, 3.0, 4.0, 6.0, -0.0, -0.5, -1.0, -1.5, -2.0, -3.0, -4.0, -6.0])


def pack_weight(w, fmt):
    k, n = w.shape
    w = f64(np.asarray(w, np.float32).astype(ml_dtypes.bfloat16)).reshape(k // 32, 32, n)
    amax = np.abs(w).max(1)
    if fmt == "e4m3":
        byte = np.frexp(amax)[1] - 1 + 127 - 7
    else:
        mant, ex = np.frexp(amax / 6.0)
        byte = np.where(mant > 0.5, ex, ex - 1) + 127
    byte = np.clip(np.where(amax > 0, byte, 1), 1, 254)
    scaled = (w * np.exp2(127.0 - byte)[:, None, :]).reshape(k, n).astype(np.float32)
    by_word = np.ascontiguousarray(scaled.reshape(k // 512, 128, 4, n).transpose(0, 1, 3, 2))
    if fmt == "e4m3":
        words = by_word.astype(ml_dtypes.float8_e4m3fn).view(np.uint8)
    else:
        c = by_word.astype(ml_dtypes.float4_e2m1fn).view(np.uint8) & 0xF
        words = (c[..., 0::2] | (c[..., 1::2] << 4)).reshape(k // 512, 128, 2 * n)
    return np.ascontiguousarray(words), np.ascontiguousarray(byte.astype(np.uint8).reshape(k // 512, 16, n))


def unpack_weight(words, scales, fmt):
    g, _, n = scales.shape
    words = np.ascontiguousarray(words).reshape(g, 128, n, -1)
    if fmt == "e4m3":
        vals = words.view(ml_dtypes.float8_e4m3fn).astype(np.float64)
    else:
        nib = np.empty((g, 128, n, 4), np.uint8)
        nib[..., 0::2] = words & 0xF
        nib[..., 1::2] = words >> 4
        vals = E2M1[nib]
    vals = vals * np.repeat(np.exp2(scales.astype(np.float64) - 127.0), 8, axis=1)[..., None]
    return vals.transpose(0, 1, 3, 2).reshape(g * 512, n)


def gelu(v):
    return 0.5 * v * (1.0 + np.tanh(np.sqrt(2.0 / np.pi) * (v + 0.044715 * v**3)))


K, H, N, T, S, T2, P = 1024, 512, 384, 4096, 1024, 2048, 1024

def setup_inputs():
    n = np.random.standard_normal
    s = mx_kscale(K)[:, None]
    u = mx_kscale(H)[:, None]
    tab_words, tab_scales = pack_weight(n((K, T)) * s, "e4m3")
    w2_words, w2_scales = pack_weight(n((K, H)) / np.sqrt(K) / s, "e2m1")
    w3_words, w3_scales = pack_weight(n((K, H)) / np.sqrt(K) / s * u.T, "e4m3")
    return {
        "tab_words": tab_words, "tab_scales": tab_scales,
        "offs": striped(np.random.permutation(T)[:S]),
        "w1": (n((K, H)) / np.sqrt(K) / s * u.T).astype(np.float32),
        "w2_words": w2_words, "w2_scales": w2_scales,
        "w3_words": w3_words, "w3_scales": w3_scales,
        "offs2": striped(np.random.permutation(T2)[:S]),
        "wgs": np.exp(0.3 * n((128, S))).astype(np.float32),
        "load": (n((H, T2)) * u).astype(np.float32),
        "w4": (n((H, N)) / np.sqrt(H) / u).astype(np.float32),
        "offs3": striped(np.random.permutation(T2)[:P]),
        "cart": np.random.uniform(0.5, 2.0, (N, P)).astype(np.float32),
        "offs4": striped(np.random.permutation(T2)[:P]),
        "wgo": np.exp(0.3 * n((128, P))).astype(np.float32),
    }

def reference(tab_words, tab_scales, offs, w1, w2_words, w2_scales, w3_words, w3_scales,
              offs2, wgs, load, w4, offs3, cart, offs4, wgo):
    v = unpack_weight(tab_words, tab_scales, "e4m3")[:, unstriped(offs)]
    a = mxq(f64(w1), 0, "e4m3").T @ v
    b = unpack_weight(w2_words, w2_scales, "e2m1").T @ v
    d = unpack_weight(w3_words, w3_scales, "e4m3").T @ v
    h = a * b - d
    page = np.zeros((H, T2))
    page[:, unstriped(offs2)] = np.tile(f64(wgs), (H // 128, 1)) * h
    z = page + f64(load)
    y = mxq(f64(w4), 0, "e4m3").T @ mxq(z, 0, "e4m3")
    x = y[:, unstriped(offs3)] / f64(cart)
    out = np.zeros((N, T2))
    out[:, unstriped(offs4)] = np.tile(f64(wgo), (N // 128, 1)) * x
    return out

from contextlib import ExitStack

import concourse.mybir as mybir
from concourse.masks import make_identity

K, H, N, T, S, T2, PICK = 1024, 512, 384, 4096, 1024, 2048, 1024
FLOPS = 2 * (3 * K * H * S + H * N * T2)

F32 = mybir.dt.float32
BF16 = mybir.dt.bfloat16
I32 = mybir.dt.int32
U32 = mybir.dt.uint32
U16 = mybir.dt.uint16
U8 = mybir.dt.uint8
FP8X4 = mybir.dt.float8_e4m3fn_x4
FP4X4 = mybir.dt.float4_e2m1fn_x4
MULT = mybir.AluOpType.mult
SUB = mybir.AluOpType.subtract
ACT = mybir.ActivationFunctionType

P = 128
PACK = 4
PASSES = K // (P * PACK)
BANK = 512
PAGES = H // P
HALVES = S // BANK
CHUNKS = T2 // BANK
OUTS = N // P
TILES = BANK // P


def tile_list_tray_cart_features_kernel(tc, tab_words, tab_scales, offs, w1, w2_words, w2_scales, w3_words,
                                                  w3_scales, offs2, wgs, load, w4, offs3, cart, offs4, wgo, out):
    nc = tc.nc
    with ExitStack() as ctx:
        lists = ctx.enter_context(tc.tile_pool(name="lists", bufs=1))
        sb = ctx.enter_context(tc.tile_pool(name="sb", bufs=1))
        psum = ctx.enter_context(tc.psum_pool(name="psum", bufs=1))

        def tile(shape, dtype, tag, bufs=1):
            return sb.tile(shape, dtype, name=tag, tag=tag, bufs=bufs, align_bytes=64)

        def bank(b):
            return psum.tile([P, BANK], F32, name=f"bank{b}", tag=f"bank{b}")

        def load_list(src, name):
            dst = lists.tile([P, src.shape[1]], U16, name=name)
            nc.sync.dma_start(dst[:], src)
            return dst

        def clear(page):
            for q in range(CHUNKS):
                nc.gpsimd.memset(page[:, q * BANK:(q + 1) * BANK], 0.0)

        tab_planes = tile([P, T // 4], I32, "tab_planes")
        nc.vector.memset(tab_planes[:], 0)
        w2_planes = tile([P, PASSES, H], U8, "w2_planes")
        w3_planes = tile([P, PASSES, H], U8, "w3_planes")
        planes1 = tile([P, S], U8, "planes1")
        nc.gpsimd.memset(w2_planes[:].bitcast(I32), 0)
        nc.gpsimd.memset(w3_planes[:].bitcast(I32), 0)
        nc.vector.memset(planes1[:].bitcast(I32), 0)
        pages = [tile([P, T2], F32, "page_even")]
        nc.vector.memset(pages[0][:], 0.0)

        w1_rows = w1.rearrange("(a p j) c -> a p j c", a=PASSES, j=PACK)
        w1_first = tile([P, PASSES, PACK, P], F32, "w1_first")
        for a in range(PASSES):
            nc.sync.dma_start(w1_first[:, a, :, :], w1_rows[a][:, :, 0:P])
        idx = load_list(offs, "idx")
        tabs = [tile([P, T], I32, f"tab{a}") for a in range(PASSES)]
        nc.sync.dma_start(tabs[0][:], tab_words[0].rearrange("p t i -> p (t i)").bitcast(I32))
        for q in range(4):
            nc.sync.dma_start(tab_planes[32 * q:32 * q + 8, :], tab_scales.bitcast(I32)[:, 4 * q:4 * q + 4, :])
        for planes, scales in ((w2_planes, w2_scales), (w3_planes, w3_scales)):
            for q in range(4):
                nc.gpsimd.dma_start(planes[:].bitcast(I32)[32 * q:32 * q + 4, :, :],
                                    scales.bitcast(I32)[:, 4 * q:4 * q + 4, :].rearrange("a r c -> r a c"))
        w3_rows = w3_words.rearrange("a p c i -> p a (c i)").bitcast(I32)
        w3_first = tile([P, PASSES, P], U32, "w3_first")
        nc.sync.dma_start(w3_first[:].bitcast(I32), w3_rows[:, :, 0:P])
        w2_codes = tile([P, PASSES, 2 * H], U8, "w2_codes")
        nc.sync.dma_start(w2_codes[:].bitcast(I32), w2_words.bitcast(I32).rearrange("a p w -> p a w"))
        nc.sync.dma_start(tabs[1][:], tab_words[1].rearrange("p t i -> p (t i)").bitcast(I32))
        w1_second = tile([P, PASSES, PACK, P], F32, "w1_second")
        for a in range(PASSES):
            nc.sync.dma_start(w1_second[:, a, :, :], w1_rows[a][:, :, P:2 * P])
        wgs_sb = tile([P, S], F32, "wgs")
        nc.sync.dma_start(wgs_sb[:], wgs)
        idx2 = load_list(offs2, "idx2")
        w3_rest = tile([P, PASSES, H - P], U32, "w3_rest")
        nc.sync.dma_start(w3_rest[:].bitcast(I32), w3_rows[:, :, P:H])
        w1_rest = tile([P, PASSES, PACK, H - 2 * P], F32, "w1_rest")
        for a in range(PASSES):
            nc.sync.dma_start(w1_rest[:, a, :, :], w1_rows[a][:, :, 2 * P:H])
        loads = [tile([P, T2], F32, f"load{c}") for c in range(PAGES)]
        carts = [tile([P, PICK], F32, f"cart{n}") for n in range(OUTS)]
        w4_raw = tile([P, PACK, N], F32, "w4_raw")
        wgo_sb = tile([P, PICK], F32, "wgo")
        for c in range(PAGES):
            nc.sync.dma_start(loads[c][:], load[c * P:(c + 1) * P, :])
            if c < OUTS:
                nc.sync.dma_start(carts[c][:], cart[c * P:(c + 1) * P, :])
            if c == 0:
                nc.sync.dma_start(w4_raw[:], w4.rearrange("(p j) n -> p j n", j=PACK))
        nc.sync.dma_start(wgo_sb[:], wgo)
        idx3 = load_list(offs3, "idx3")
        idx4 = load_list(offs4, "idx4")

        ident = tile([P, P], F32, "ident")
        make_identity(nc, ident[:])

        def quantize_w1(c):
            raw = (w1_first, w1_second)[c][:] if c < 2 else w1_rest[:, :, :, (c - 2) * P:(c - 1) * P]
            grouped = tile([P, PASSES * P * PACK], BF16, f"feats{(c + 1) % 2}")
            nc.scalar.copy(grouped[:].rearrange("p (a c i j) -> p a c j i", a=PASSES, i=4, j=PACK),
                           raw.rearrange("p a j (c i) -> p a c j i", i=4))
            codes = tile([P, PASSES * P], U32, f"w1_codes{c}")
            planes = tile([P, PASSES * P], U8, f"w1_planes{c}")
            nc.vector.quantize_mx(codes[:].bitcast(FP8X4), planes[:], grouped[:])
            return codes, planes

        w1_mx = [quantize_w1(0)]

        planes0 = tile([P, S], U8, "planes0")
        nc.vector.tensor_copy(planes0[:], tab_planes[:].bitcast(U8).indirect(idx[:]))
        nc.gpsimd.dma_start(planes1[:].bitcast(I32)[0:112, :], planes0[:].bitcast(I32)[4:116, :])
        cols = BANK // 16
        picked = {}
        for a in range(PASSES):
            for h in range(HALVES):
                picked[a, h] = tile([P, BANK], U32, f"picked{a}{h}")
                nc.vector.tensor_copy(picked[a, h][:], tabs[a][:].bitcast(U32).indirect(idx[:, h * cols:(h + 1) * cols]))

        def project(c, h):
            j = slice(h * BANK, (h + 1) * BANK)
            acc_a, acc_b, acc_d = bank(3 * h), bank(3 * h + 1), bank(3 * h + 2)
            codes, planes = w1_mx[c]
            w3_codes = w3_first[:] if c == 0 else w3_rest[:, :, (c - 1) * P:c * P]
            for a in range(PASSES):
                nc.tensor.matmul_mx(acc_a[:], lhsT=codes[:, a * P:(a + 1) * P].bitcast(FP8X4),
                                    lhsT_scale=planes[:, a * P:(a + 1) * P],
                                    rhs=picked[a, h][:].bitcast(FP8X4), rhs_scale=planes0[4 * a:P, j],
                                    start=(a == 0), stop=(a == PASSES - 1))
            for a in range(PASSES):
                nc.tensor.matmul_mx(acc_b[:], lhsT=w2_codes[:, a, 2 * c * P:2 * (c + 1) * P].bitcast(FP4X4),
                                    lhsT_scale=w2_planes[:, a, c * P:(c + 1) * P],
                                    rhs=picked[a, h][:].bitcast(FP8X4), rhs_scale=(planes0, planes1)[a][:, j],
                                    start=(a == 0), stop=(a == PASSES - 1))
            for a in range(PASSES):
                nc.tensor.matmul_mx(acc_d[:], lhsT=w3_codes[:, a, :].bitcast(FP8X4),
                                    lhsT_scale=w3_planes[:, a, c * P:(c + 1) * P],
                                    rhs=picked[a, h][:].bitcast(FP8X4), rhs_scale=planes0[4 * a:P, j],
                                    start=(a == 0), stop=(a == PASSES - 1))
            a_sb = tile([P, BANK], F32, f"a_sb{h}")
            nc.scalar.copy(a_sb[:], acc_a[:])
            return a_sb, acc_b, acc_d

        z_turned = [tile([P, TILES, 2, P, 2], BF16, f"z_turned{q}") for q in range(CHUNKS)]

        def turn_page(c, q, b, copy):
            acc = bank(b)
            for s, src in enumerate((loads[c], pages[c])):
                for i in range(TILES):
                    t0 = q * BANK + i * P
                    nc.tensor.matmul(acc[:, i * P:(i + 1) * P], lhsT=src[:, t0:t0 + P], rhs=ident[:], is_transpose=True,
                                     start=(s == 0 and i == 0), stop=(s == 1 and i == TILES - 1))
            copy(z_turned[q][:, :, :, 32 * c:32 * (c + 1), :],
                 acc[:].rearrange("t (i p u e) -> t i u p e", i=TILES, u=2, e=2))

        outs = []
        inverses = []
        pages.append(tile([P, T2], F32, "tab1"))
        clear(pages[1])
        parts = [project(0, h) for h in range(HALVES)]
        for c in range(PAGES):
            if c + 1 < PAGES:
                w1_mx.append(quantize_w1(c + 1))
            feats = tile([P, S], F32, f"feats{c % 2}")
            prods = []
            for h in range(HALVES):
                prod = tile([P, BANK], F32, "prod", bufs=2)
                nc.vector.tensor_tensor(prod[:], parts[h][1][:], parts[h][0][:], MULT)
                prods.append(prod)
            for h in range(HALVES):
                nc.vector.tensor_tensor(feats[:, h * BANK:(h + 1) * BANK], prods[h][:], parts[h][2][:], SUB)
            if c == 0:
                for h in range(HALVES):
                    j = slice(h * BANK, (h + 1) * BANK)
                    nc.vector.tensor_tensor(pages[c][:].indirect(idx2[:, h * cols:(h + 1) * cols]), feats[:, j], wgs_sb[:, j], MULT)
            else:
                nc.vector.tensor_tensor(pages[c][:].indirect(idx2[:]), feats[:], wgs_sb[:], MULT)
            if c > 0:
                for q in range(CHUNKS):
                    turn_page(c - 1, q, (6, 7, 2, 5)[q], nc.scalar.copy)
                if c + 1 < PAGES:
                    pages.append(tile([P, T2], F32, "page_even" if c % 2 == 1 else "tab1"))
                    clear(pages[c + 1])
                outs.append(tile([P, T2], F32, f"load{c - 1}"))
                clear(outs[c - 1])
                root = tile([P, PICK], F32, "a_sb0")
                nc.scalar.activation(root[:], carts[c - 1][:], ACT.Abs_reciprocal_sqrt)
                inverses.append(tile([P, PICK], F32, f"cart{c - 1}"))
                nc.scalar.activation(inverses[c - 1][:], root[:], ACT.Square)
            if c + 1 < PAGES:
                parts = [project(c + 1, h) for h in range(HALVES)]
            else:
                for q in range(CHUNKS):
                    turn_page(c, q, (6 + q) % 8, (nc.scalar.copy, nc.vector.tensor_copy)[q % 2])
            if c == 1:
                w4_grouped = tile([P, N * PACK], BF16, "feats1")
                nc.scalar.copy(w4_grouped[:].rearrange("p (c i j) -> p c j i", i=4, j=PACK),
                               w4_raw[:].rearrange("p j (c i) -> p c j i", i=4))
                w4_codes = tile([P, N], U32, "w4_codes")
                w4_planes = tile([P, N], U8, "w4_planes")
                for n0, n1 in ((0, 2 * P), (2 * P, N)):
                    nc.vector.quantize_mx(w4_codes[:, n0:n1].bitcast(FP8X4), w4_planes[:, n0:n1],
                                          w4_grouped[:, PACK * n0:PACK * n1])

        z_codes = [tile([P, BANK], U32, f"z_codes{q}") for q in range(CHUNKS)]
        z_planes = [tile([P, BANK], U8, f"z_planes{q}") for q in range(CHUNKS)]
        ys = [tile([P, T2], F32, tag) for tag in ("tab0", "w1_rest", "load3")]

        def second(n, q, b):
            acc = bank(b)
            nc.tensor.matmul_mx(acc[:], lhsT=w4_codes[:, n * P:(n + 1) * P].bitcast(FP8X4),
                                lhsT_scale=w4_planes[:, n * P:(n + 1) * P],
                                rhs=z_codes[q][:].bitcast(FP8X4), rhs_scale=z_planes[q][:], start=True, stop=True)
            nc.scalar.copy(ys[n][:, q * BANK:(q + 1) * BANK], acc[:])

        for q in range(CHUNKS):
            words = z_turned[q][:].rearrange("t i u p e -> t i u (p e)").bitcast(F32)
            for g in range(2):
                acc = bank(2 + (2 * q + g) % 4)
                for i in range(2):
                    for u in range(2):
                        o = u * 2 * P + i * P
                        nc.tensor.transpose(acc[:, o:o + P], words[:, 2 * g + i, u, :], ident[:])
                grouped = tile([P, 2 * P * PACK], BF16, ("a_sb0", "a_sb1", "feats0", "feats1")[(2 * q + g) % 4])
                (nc.scalar.copy, nc.vector.tensor_copy)[g](
                    grouped[:].bitcast(F32).rearrange("p (t u) -> p t u", u=2),
                    acc[:].rearrange("p (u t) -> p t u", u=2))
                t = slice(g * 2 * P, (g + 1) * 2 * P)
                nc.vector.quantize_mx(z_codes[q][:, t].bitcast(FP8X4), z_planes[q][:, t], grouped[:])
            second(0, q, (6 + q) % 8)
        for n in range(1, OUTS):
            for q in range(CHUNKS):
                second(n, q, (2 + 4 * (n - 1) + q) % 8)

        for n in range(OUTS):
            done = tile([P, PICK], F32, "done", bufs=2)
            nc.vector.tensor_tensor(done[:], ys[n][:].indirect(idx3[:]), inverses[n][:], MULT)
            nc.vector.tensor_tensor(outs[n][:].indirect(idx4[:]), done[:], wgo_sb[:], MULT)
            nc.sync.dma_start(out[n * P:(n + 1) * P, :], outs[n][:])
